import numpy as np
import ml_dtypes


def mxq(x, axis, fmt="e4m3"):
    dtype, down = {"e4m3": (ml_dtypes.float8_e4m3fn, 7), "e5m2": (ml_dtypes.float8_e5m2, 14)}[fmt]
    v = np.moveaxis(np.asarray(x, np.float32).astype(ml_dtypes.bfloat16).astype(np.float64), axis, -1)
    blocks = v.reshape(v.shape[:-1] + (-1, 32))
    amax = np.abs(blocks).max(-1, keepdims=True)
    byte = np.maximum(np.where(amax > 0, np.frexp(amax)[1] - 1 + 127, 0) - down, 1)
    scale = np.exp2(byte - 127.0)
    codes = (blocks / scale).astype(np.float32).astype(dtype).astype(np.float64)
    return np.moveaxis((codes * scale).reshape(v.shape), -1, axis)


WIDE = False


def mx_kscale(k):
    if not WIDE:
        return np.ones(k)
    levels = np.array([10, -10, 5, -5, 0])
    if k % 512:
        return np.exp2(np.random.permutation(np.resize(levels, k // 32))).repeat(32)
    a = np.empty((k // 512, 16))
    for p in range(k // 512):
        a[p, :8] = np.random.permutation(np.resize(levels, 8))
        for g in range(8):
            far = levels[np.abs(levels - a[p, g]) >= 10]
            a[p, g + 8] = far[np.random.randint(len(far))]
    return np.exp2(a.ravel()).repeat(32)


def f64(x):
    return np.asarray(x).astype(np.float64)


def striped(idx):
    return np.tile(idx.reshape(-1, 16).T, (8, 1)).astype(np.uint16)


def unstriped(offs):
    return offs[:16].T.reshape(-1).astype(np.int64)


E2M1 = np.array([0.0, 0.5, 1.0, 1.5, 2.0, 3.0, 4.0, 6.0, -0.0, -0.5, -1.0, -1.5, -2.0, -3.0, -4.0, -6.0])


def pack_weight(w, fmt):
    k, n = w.shape
    w = f64(np.asarray(w, np.float32).astype(ml_dtypes.bfloat16)).reshape(k // 32, 32, n)
    amax = np.abs(w).max(1)
    if fmt == "e4m3":
        byte = np.frexp(amax)[1] - 1 + 127 - 7
    else:
        mant, ex = np.frexp(amax / 6.0)
        byte = np.where(mant > 0.5, ex, ex - 1) + 127
    byte = np.clip(np.where(amax > 0, byte, 1), 1, 254)
    scaled = (w * np.exp2(127.0 - byte)[:, None, :]).reshape(k, n).astype(np.float32)
    by_word = np.ascontiguousarray(scaled.reshape(k // 512, 128, 4, n).transpose(0, 1, 3, 2))
    if fmt == "e4m3":
        words = by_word.astype(ml_dtypes.float8_e4m3fn).view(np.uint8)
    else:
        c = by_word.astype(ml_dtypes.float4_e2m1fn).view(np.uint8) & 0xF
        words = (c[..., 0::2] | (c[..., 1::2] << 4)).reshape(k // 512, 128, 2 * n)
    return np.ascontiguousarray(words), np.ascontiguousarray(byte.astype(np.uint8).reshape(k // 512, 16, n))


def unpack_weight(words, scales, fmt):
    g, _, n = scales.shape
    words = np.ascontiguousarray(words).reshape(g, 128, n, -1)
    if fmt == "e4m3":
        vals = words.view(ml_dtypes.float8_e4m3fn).astype(np.float64)
    else:
        nib = np.empty((g, 128, n, 4), np.uint8)
        nib[..., 0::2] = words & 0xF
        nib[..., 1::2] = words >> 4
        vals = E2M1[nib]
    vals = vals * np.repeat(np.exp2(scales.astype(np.float64) - 127.0), 8, axis=1)[..., None]
    return vals.transpose(0, 1, 3, 2).reshape(g * 512, n)


def gelu(v):
    return 0.5 * v * (1.0 + np.tanh(np.sqrt(2.0 / np.pi) * (v + 0.044715 * v**3)))


K, H, T, S, T3, S2, P = 1024, 512, 4096, 1024, 2048, 1024, 512


def setup_inputs():
    n = np.random.standard_normal
    s = mx_kscale(K)[:, None]
    u = mx_kscale(H)[:, None]
    tab_words, tab_scales = pack_weight(n((K, T)) * s, "e4m3")
    tab2_words, tab2_scales = pack_weight(0.8 * n((H, T3)) / np.sqrt(H) / u, "e4m3")
    w2_words, w2_scales = pack_weight(n((K, H)) / np.sqrt(K) / s, "e2m1")
    return {
        "tab_words": tab_words,
        "tab_scales": tab_scales,
        "offs": striped(np.random.permutation(T)[:S]),
        "tab2_words": tab2_words,
        "tab2_scales": tab2_scales,
        "offs2": striped(np.random.permutation(T3)[:S2]),
        "pos1": striped(np.random.permutation(S)[:P]),
        "pos2": striped(np.random.permutation(S)[:P]),
        "w1": (n((K, H)) / np.sqrt(K) / s * u.T).astype(np.float32),
        "w2_words": w2_words,
        "w2_scales": w2_scales,
        "w3": (n((K, H)) / np.sqrt(K) / s * u.T).astype(np.float32),
        "temp": np.random.uniform(0.4, 1.6, S2).astype(np.float32),
        "lean": (0.5 * n(S2)).astype(np.float32),
    }


def reference(tab_words, tab_scales, offs, tab2_words, tab2_scales, offs2, pos1, pos2,
              w1, w2_words, w2_scales, w3, temp, lean):
    v = unpack_weight(tab_words, tab_scales, "e4m3")[:, unstriped(offs)]
    v2 = unpack_weight(tab2_words, tab2_scales, "e4m3")[:, unstriped(offs2)]
    w2 = unpack_weight(w2_words, w2_scales, "e2m1")
    f = mxq(f64(w1), 0, "e4m3").T @ v
    b = w2.T @ v
    d = mxq(f64(w3), 0, "e4m3").T @ v
    h = np.maximum(f * b, d)
    e = v2.T @ mxq(h, 0, "e4m3")
    top = e.max(axis=1)
    a = np.exp(f64(temp)[:, None] * (e[:, unstriped(pos1)] - top[:, None]))
    c = e[:, unstriped(pos2)]
    return 5.0 * a * c + f64(lean)[:, None]

@@ -1,0 +1,245 @@
+from contextlib import ExitStack
+
+import concourse.mybir as mybir
+
+K, H, T, S, T3, S2, NP = 1024, 512, 4096, 1024, 2048, 1024, 512
+FLOPS = 2 * (3 * K * H * S + H * S2 * S)
+
+F32 = mybir.dt.float32
+BF16 = mybir.dt.bfloat16
+I32 = mybir.dt.int32
+U32 = mybir.dt.uint32
+U16 = mybir.dt.uint16
+U8 = mybir.dt.uint8
+FP8X4 = mybir.dt.float8_e4m3fn_x4
+FP4X4 = mybir.dt.float4_e2m1fn_x4
+ALU = mybir.AluOpType
+ACT = mybir.ActivationFunctionType
+
+P = 128
+PACK = 4
+PASSES = K // (P * PACK)
+BLK = 128
+NBLK = S // BLK
+HALF = 512
+MT = S2 // P
+
+
+def tile_list_cousin_segment_scores_kernel(
+    tc, tab_words, tab_scales, offs, tab2_words, tab2_scales, offs2, pos1, pos2,
+    w1, w2_words, w2_scales, w3, temp, lean, out,
+):
+    nc = tc.nc
+    with ExitStack() as ctx:
+        lists = ctx.enter_context(tc.tile_pool(name="lists", bufs=1))
+        keep = ctx.enter_context(tc.tile_pool(name="keep", bufs=1))
+        ring = ctx.enter_context(tc.tile_pool(name="ring", bufs=4))
+        psum = ctx.enter_context(tc.psum_pool(name="psum", bufs=8))
+
+        def kept(name, shape, dtype):
+            return keep.tile(shape, dtype, name=name, align_bytes=64)
+
+        offs_sb = lists.tile([P, S // 16], U16, name="offs_sb")
+        offs2_sb = lists.tile([P, S2 // 16], U16, name="offs2_sb")
+        pos1_sb = lists.tile([P, NP // 16], U16, name="pos1_sb")
+        pos2_sb = lists.tile([P, NP // 16], U16, name="pos2_sb")
+
+        tab_w = [kept("tab_w%d" % a, [P, T], U32) for a in range(PASSES)]
+        tab_s = kept("tab_s", [P, T], U8)
+        tab2_w = kept("tab2_w", [P, T3], U32)
+        tab2_s = kept("tab2_s", [P, T3], U8)
+        w2_w_raw = kept("w2_w_raw", [P, PASSES, 2 * H], U8)
+        w2_s_raw = kept("w2_s_raw", [P, PASSES, H], U8)
+        v_s1 = kept("v_s1", [P, S], U8)
+
+        nc.vector.memset(tab_s[:].bitcast(I32), 0)
+        nc.vector.memset(tab2_s[:].bitcast(I32), 0)
+        nc.vector.memset(w2_s_raw[:].bitcast(I32), 0)
+        nc.vector.memset(v_s1[:].bitcast(I32), 0)
+
+        def load_words(dst, src, c0, c1):
+            nc.sync.dma_start(dst[:, c0:c1].bitcast(I32),
+                              src[:, c0:c1, :].rearrange("p t i -> p (t i)").bitcast(I32))
+
+        def load_weight(name, w, a, c0, c1):
+            raw = kept(name, [P, PACK, c1 - c0], F32)
+            rows = w[a * P * PACK:(a + 1) * P * PACK, c0:c1]
+            nc.sync.dma_start(raw[:], rows.rearrange("(p j) c -> p j c", j=PACK))
+            return raw
+
+        def load_scale_rows(dst, src):
+            nc.sync.dma_start(dst.bitcast(I32), src.bitcast(I32))
+
+        def load_w2_scales(q):
+            load_scale_rows(w2_s_raw[32 * q:32 * q + 4, :, :],
+                            w2_scales[:, 4 * q:4 * q + 4, :].rearrange("a r c -> r a c"))
+
+        nc.sync.dma_start(offs_sb[:], offs)
+        nc.sync.dma_start(w2_w_raw[:].bitcast(I32), w2_words.rearrange("a p c -> p a c").bitcast(I32))
+        nc.sync.dma_start(offs2_sb[:], offs2)
+        nc.sync.dma_start(pos1_sb[:], pos1)
+        nc.sync.dma_start(pos2_sb[:], pos2)
+        for q in range(3):
+            load_words(tab_w[0], tab_words[0], q * T // 4, (q + 1) * T // 4)
+        for r in range(4):
+            load_scale_rows(tab_s[r:P:16, :], tab_scales[:, r:16:4, :].rearrange("a q t -> q a t"))
+        load_w2_scales(0)
+        load_words(tab_w[0], tab_words[0], 3 * T // 4, T)
+        for q in range(1, 4):
+            load_w2_scales(q)
+        w1_raw0 = load_weight("w1_raw0", w1, 0, 0, H)
+        for q in range(4):
+            load_scale_rows(tab2_s[32 * q:32 * q + 4, :], tab2_scales[0, 4 * q:4 * q + 4, :])
+        load_words(tab_w[1], tab_words[1], 0, T)
+        w1_raw1a = load_weight("w1_raw1a", w1, 1, 0, H // 2)
+        w1_raw1b = load_weight("w1_raw1b", w1, 1, H // 2, H)
+        w3_raw0 = load_weight("w3_raw0", w3, 0, 0, H)
+        w3_raw1a = load_weight("w3_raw1a", w3, 1, 0, H // 2)
+        w3_raw1b = load_weight("w3_raw1b", w3, 1, H // 2, H)
+        load_words(tab2_w, tab2_words[0], 0, T3)
+        temp_sb = kept("temp_sb", [P, MT], F32)
+        lean_sb = kept("lean_sb", [P, MT], F32)
+        with nc.allow_non_contiguous_dma(reason="one value a row, rows on partitions"):
+            nc.sync.dma_start(temp_sb[:], temp.rearrange("(c p) -> p c", p=P))
+            nc.sync.dma_start(lean_sb[:], lean.rearrange("(c p) -> p c", p=P))
+
+        def round_weight(copy, grouped, raw, c0, c1):
+            dst = grouped[:].rearrange("p (t m j) -> p m j t", t=PACK, j=PACK)[:, c0 // PACK:c1 // PACK]
+            copy(dst, raw[:].rearrange("p j (m t) -> p m j t", t=PACK))
+
+        def quantise(name, grouped, width):
+            codes = kept(name + "_c", [P, width], U32)
+            scales = kept(name + "_s", [P, width], U8)
+            nc.vector.quantize_mx(out=codes[:].bitcast(FP8X4), scales=scales[:], in_=grouped)
+            return codes, scales
+
+        w2_w = kept("w2_w", [P, PASSES, 2 * H], U8)
+        w2_s = kept("w2_s", [P, PASSES, H], U8)
+        nc.vector.tensor_copy(w2_w[:].bitcast(U16).rearrange("p a (t m) -> p a t m", t=PACK),
+                              w2_w_raw[:].bitcast(U16).rearrange("p a (m t) -> p a t m", t=PACK))
+        v_s0 = kept("v_s0", [P, S], U8)
+        nc.vector.tensor_copy(v_s0[:], tab_s[:].indirect(offs_sb[:]))
+        nc.scalar.dma_start(v_s1[0:P - 16, :].bitcast(I32), v_s0[16:P, :].bitcast(I32))
+        v_s = [v_s0, v_s1]
+        v_w = [kept("v_w%d" % a, [P, S], U32) for a in range(PASSES)]
+        nc.vector.tensor_copy(v_w[0][:], tab_w[0][:].indirect(offs_sb[:]))
+        nc.vector.tensor_copy(w2_s[:].rearrange("p a (t m) -> p a t m", t=PACK),
+                              w2_s_raw[:].rearrange("p a (m t) -> p a t m", t=PACK))
+        v2_s = kept("v2_s", [P, S2], U8)
+        nc.vector.tensor_copy(v2_s[:], tab2_s[:].indirect(offs2_sb[:]))
+
+        w1_g = [kept("w1_g%d" % a, [P, PACK * H], BF16) for a in range(PASSES)]
+        w3_g = [kept("w3_g%d" % a, [P, PACK * H], BF16) for a in range(PASSES)]
+        round_weight(nc.scalar.copy, w1_g[0], w1_raw0, 0, H)
+        w1_q = [quantise("w1q0", w1_g[0][:], H)]
+        for h in range(2):
+            nc.vector.tensor_copy(v_w[1][:, h * HALF:(h + 1) * HALF],
+                                  tab_w[1][:].indirect(offs_sb[:, h * 32:(h + 1) * 32]))
+        round_weight(nc.scalar.copy, w1_g[1], w1_raw1a, 0, H // 2)
+        round_weight(nc.vector.tensor_copy, w1_g[1], w1_raw1b, H // 2, H)
+        w1_q.append(quantise("w1q1", w1_g[1][:], H))
+
+        def first_stage_pass(bank, codes, scales, a, c, t, start, stop):
+            cols = slice(c * BLK, (c + 1) * BLK)
+            nc.tensor.matmul_mx(out=bank[:, t, :], lhsT=codes, lhsT_scale=scales,
+                                rhs=v_w[a][:, cols].bitcast(FP8X4),
+                                rhs_scale=v_s[a][:, cols],
+                                start=start, stop=stop)
+
+        def fp8_side(q, a, t):
+            return q[a][0][:, t * P:(t + 1) * P].bitcast(FP8X4), q[a][1][:, t * P:(t + 1) * P]
+
+        def fp4_side(a, t):
+            return w2_w[:, a, 2 * t * P:2 * (t + 1) * P].bitcast(FP4X4), w2_s[:, a, t * P:(t + 1) * P]
+
+        def woven(bank):
+            return bank[:].rearrange("p t n -> p n t")
+
+        def block(tile_, c):
+            return tile_[:, c * BLK * PACK:(c + 1) * BLK * PACK].rearrange("p (n t) -> p n t", t=PACK)
+
+        b_sb = kept("b_sb", [P, S * PACK], F32)
+        b_banks = []
+        for c in range(NBLK):
+            bank = psum.tile([P, PACK, BLK], F32, name="bank")
+            for t in range(PACK):
+                first_stage_pass(bank, *fp4_side(0, t), 0, c, t, t == 0, False)
+            b_banks.append(bank)
+        for c in range(NBLK):
+            for t in range(PACK):
+                first_stage_pass(b_banks[c], *fp4_side(1, t), 1, c, t, False, t == PACK - 1)
+            nc.scalar.copy(block(b_sb, c), woven(b_banks[c]))
+
+        fb_sb = kept("fb_sb", [P, S * PACK], F32)
+        for c in range(NBLK):
+            bank = psum.tile([P, PACK, BLK], F32, name="bank")
+            for t in range(PACK):
+                for a in range(PASSES):
+                    first_stage_pass(bank, *fp8_side(w1_q, a, t), a, c, t, a == 0, a == PASSES - 1)
+            nc.vector.tensor_tensor(block(fb_sb, c), woven(bank), block(b_sb, c), ALU.mult)
+
+        round_weight(nc.scalar.copy, w3_g[0], w3_raw0, 0, H)
+        round_weight(nc.scalar.copy, w3_g[1], w3_raw1a, 0, H // 2)
+        round_weight(nc.scalar.copy, w3_g[1], w3_raw1b, H // 2, H)
+        w3_q = [quantise("w3q0", w3_g[0][:], H), quantise("w3q1", w3_g[1][:], H)]
+
+        v2_w = kept("v2_w", [P, S2], U32)
+        for h in range(2):
+            nc.vector.tensor_copy(v2_w[:, h * HALF:(h + 1) * HALF],
+                                  tab2_w[:].indirect(offs2_sb[:, h * 32:(h + 1) * 32]))
+
+        d_banks = []
+        for c in range(NBLK):
+            bank = psum.tile([P, PACK, BLK], F32, name="bank")
+            for t in range(PACK):
+                first_stage_pass(bank, *fp8_side(w3_q, 0, t), 0, c, t, t == 0, False)
+            d_banks.append(bank)
+        h_g = [kept("h_g%d" % h, [P, HALF * PACK], BF16) for h in range(2)]
+        h_q = []
+        for c in range(NBLK):
+            bank = d_banks[c]
+            for t in range(PACK):
+                first_stage_pass(bank, *fp8_side(w3_q, 1, t), 1, c, t, False, t == PACK - 1)
+            nc.vector.tensor_tensor(block(h_g[c // 4], c % 4), woven(bank), block(fb_sb, c), ALU.max)
+            if c % 4 == 3:
+                h_q.append(quantise("hq%d" % (c // 4), h_g[c // 4][:], HALF))
+
+        neg_temp = kept("neg_temp", [P, MT], F32)
+        nc.scalar.mul(neg_temp[:], temp_sb[:], -1.0)
+        top_half = kept("top_half", [P, MT], F32)
+        top = kept("top", [P, MT], F32)
+        bias = kept("bias", [P, MT], F32)
+
+        def scores(m):
+            rows = slice(m * P, (m + 1) * P)
+            col = slice(m, m + 1)
+            e_sb = kept("e_sb%d" % m, [P, S], F32)
+            for h in range(2):
+                bank = psum.tile([P, HALF], F32, name="bank")
+                nc.tensor.matmul_mx(out=bank[:], lhsT=v2_w[:, rows].bitcast(FP8X4), lhsT_scale=v2_s[:, rows],
+                                    rhs=h_q[h][0][:].bitcast(FP8X4), rhs_scale=h_q[h][1][:],
+                                    start=True, stop=True)
+                nc.vector.tensor_scalar(out=e_sb[:, h * HALF:(h + 1) * HALF], in0=bank[:], scalar1=1.0,
+                                        scalar2=None if h == 0 else top_half[:, col],
+                                        op0=ALU.mult, op1=ALU.max,
+                                        accum_out=(top_half if h == 0 else top)[:, col])
+            nc.scalar.activation(out=bias[:, col], in_=top[:, col], func=ACT.Copy, scale=neg_temp[:, col])
+            look = ring.tile([P, NP], F32, name="look")
+            nc.scalar.activation(out=look[:], in_=e_sb[:].indirect(pos1_sb[:]), func=ACT.Exp,
+                                 bias=bias[:, col], scale=temp_sb[:, col])
+            return e_sb, look
+
+        def features(m, e_sb, look):
+            prod = ring.tile([P, NP], F32, name="prod")
+            nc.vector.tensor_tensor(prod[:], e_sb[:].indirect(pos2_sb[:]), look[:], ALU.mult)
+            res = ring.tile([P, NP], F32, name="res")
+            nc.scalar.activation(out=res[:], in_=prod[:], func=ACT.Identity, scale=5.0,
+                                 bias=lean_sb[:, m:m + 1])
+            nc.sync.dma_start(out[m * P:(m + 1) * P, :], res[:])
+
+        pending = scores(0)
+        for m in range(1, MT):
+            ahead = scores(m)
+            features(m - 1, *pending)
+            pending = ahead
+        features(MT - 1, *pending)

@@ -33,6 +33,8 @@ def tile_list_cousin_segment_scores_kernel(
     with ExitStack() as ctx:
         lists = ctx.enter_context(tc.tile_pool(name="lists", bufs=1))
         keep = ctx.enter_context(tc.tile_pool(name="keep", bufs=1))
+        shared = ctx.enter_context(tc.tile_pool(name="shared", bufs=1))
+        stage = ctx.enter_context(tc.tile_pool(name="stage", bufs=1))
         ring = ctx.enter_context(tc.tile_pool(name="ring", bufs=4))
         psum = ctx.enter_context(tc.psum_pool(name="psum", bufs=8))
 
@@ -44,7 +46,7 @@ def tile_list_cousin_segment_scores_kernel(
         pos1_sb = lists.tile([P, NP // 16], U16, name="pos1_sb")
         pos2_sb = lists.tile([P, NP // 16], U16, name="pos2_sb")
 
-        tab_w = [kept("tab_w%d" % a, [P, T], U32) for a in range(PASSES)]
+        tab_w = [kept("tab_w0", [P, T], U32), shared.tile([P, T], U32, name="tab_w1", offset=0)]
         tab_s = kept("tab_s", [P, T], U8)
         tab2_w = kept("tab2_w", [P, T3], U32)
         tab2_s = kept("tab2_s", [P, T3], U8)
@@ -80,23 +82,29 @@ def tile_list_cousin_segment_scores_kernel(
         nc.sync.dma_start(pos1_sb[:], pos1)
         nc.sync.dma_start(pos2_sb[:], pos2)
         for q in range(3):
-            load_words(tab_w[0], tab_words[0], q * T // 4, (q + 1) * T // 4)
+            load_words(tab_w[0], tab_words[0], q * T // 16, (q + 1) * T // 16)
         for r in range(4):
             load_scale_rows(tab_s[r:P:16, :], tab_scales[:, r:16:4, :].rearrange("a q t -> q a t"))
-        load_w2_scales(0)
-        load_words(tab_w[0], tab_words[0], 3 * T // 4, T)
-        for q in range(1, 4):
+        load_words(tab_w[0], tab_words[0], 3 * T // 16, T)
+        for q in range(4):
             load_w2_scales(q)
         w1_raw0 = load_weight("w1_raw0", w1, 0, 0, H)
         for q in range(4):
             load_scale_rows(tab2_s[32 * q:32 * q + 4, :], tab2_scales[0, 4 * q:4 * q + 4, :])
-        load_words(tab_w[1], tab_words[1], 0, T)
-        w1_raw1a = load_weight("w1_raw1a", w1, 1, 0, H // 2)
-        w1_raw1b = load_weight("w1_raw1b", w1, 1, H // 2, H)
+        load_words(tab_w[1], tab_words[1], 0, T // 2)
+        w2_w = kept("w2_w", [P, PASSES, 2 * H], U8)
+        w2_s = kept("w2_s", [P, PASSES, H], U8)
+        nc.vector.tensor_copy(w2_w[:].bitcast(U16).rearrange("p a (t m) -> p a t m", t=PACK),
+                              w2_w_raw[:].bitcast(U16).rearrange("p a (m t) -> p a t m", t=PACK))
+        v_s0 = kept("v_s0", [P, S], U8)
+        nc.vector.tensor_copy(v_s0[:], tab_s[:].indirect(offs_sb[:]))
+        nc.sync.dma_start(v_s1[0:P - 16, :].bitcast(I32), v_s0[16:P, :].bitcast(I32))
+        load_words(tab_w[1], tab_words[1], T // 2, T)
+        w1_raw1 = load_weight("w1_raw1", w1, 1, 0, H)
+        load_words(tab2_w, tab2_words[0], 0, T3)
         w3_raw0 = load_weight("w3_raw0", w3, 0, 0, H)
         w3_raw1a = load_weight("w3_raw1a", w3, 1, 0, H // 2)
         w3_raw1b = load_weight("w3_raw1b", w3, 1, H // 2, H)
-        load_words(tab2_w, tab2_words[0], 0, T3)
         temp_sb = kept("temp_sb", [P, MT], F32)
         lean_sb = kept("lean_sb", [P, MT], F32)
         with nc.allow_non_contiguous_dma(reason="one value a row, rows on partitions"):
@@ -113,13 +121,6 @@ def tile_list_cousin_segment_scores_kernel(
             nc.vector.quantize_mx(out=codes[:].bitcast(FP8X4), scales=scales[:], in_=grouped)
             return codes, scales
 
-        w2_w = kept("w2_w", [P, PASSES, 2 * H], U8)
-        w2_s = kept("w2_s", [P, PASSES, H], U8)
-        nc.vector.tensor_copy(w2_w[:].bitcast(U16).rearrange("p a (t m) -> p a t m", t=PACK),
-                              w2_w_raw[:].bitcast(U16).rearrange("p a (m t) -> p a t m", t=PACK))
-        v_s0 = kept("v_s0", [P, S], U8)
-        nc.vector.tensor_copy(v_s0[:], tab_s[:].indirect(offs_sb[:]))
-        nc.scalar.dma_start(v_s1[0:P - 16, :].bitcast(I32), v_s0[16:P, :].bitcast(I32))
         v_s = [v_s0, v_s1]
         v_w = [kept("v_w%d" % a, [P, S], U32) for a in range(PASSES)]
         nc.vector.tensor_copy(v_w[0][:], tab_w[0][:].indirect(offs_sb[:]))
@@ -128,15 +129,14 @@ def tile_list_cousin_segment_scores_kernel(
         v2_s = kept("v2_s", [P, S2], U8)
         nc.vector.tensor_copy(v2_s[:], tab2_s[:].indirect(offs2_sb[:]))
 
-        w1_g = [kept("w1_g%d" % a, [P, PACK * H], BF16) for a in range(PASSES)]
-        w3_g = [kept("w3_g%d" % a, [P, PACK * H], BF16) for a in range(PASSES)]
+        w1_g = [kept("w1_g0", [P, PACK * H], BF16),
+                shared.tile([P, PACK * H], BF16, name="w1_g1", offset=0, align_bytes=64)]
         round_weight(nc.scalar.copy, w1_g[0], w1_raw0, 0, H)
         w1_q = [quantise("w1q0", w1_g[0][:], H)]
         for h in range(2):
             nc.vector.tensor_copy(v_w[1][:, h * HALF:(h + 1) * HALF],
                                   tab_w[1][:].indirect(offs_sb[:, h * 32:(h + 1) * 32]))
-        round_weight(nc.scalar.copy, w1_g[1], w1_raw1a, 0, H // 2)
-        round_weight(nc.vector.tensor_copy, w1_g[1], w1_raw1b, H // 2, H)
+        round_weight(nc.vector.tensor_copy, w1_g[1], w1_raw1, 0, H)
         w1_q.append(quantise("w1q1", w1_g[1][:], H))
 
         def first_stage_pass(bank, codes, scales, a, c, t, start, stop):
@@ -158,7 +158,8 @@ def tile_list_cousin_segment_scores_kernel(
         def block(tile_, c):
             return tile_[:, c * BLK * PACK:(c + 1) * BLK * PACK].rearrange("p (n t) -> p n t", t=PACK)
 
-        b_sb = kept("b_sb", [P, S * PACK], F32)
+        b_sb = [stage.tile([P, BLK, PACK], F32, name="b_sb%d" % c, offset=2048 * c, align_bytes=64)
+                for c in range(NBLK)]
         b_banks = []
         for c in range(NBLK):
             bank = psum.tile([P, PACK, BLK], F32, name="bank")
@@ -168,25 +169,26 @@ def tile_list_cousin_segment_scores_kernel(
         for c in range(NBLK):
             for t in range(PACK):
                 first_stage_pass(b_banks[c], *fp4_side(1, t), 1, c, t, False, t == PACK - 1)
-            nc.scalar.copy(block(b_sb, c), woven(b_banks[c]))
+            nc.scalar.copy(b_sb[c][:], woven(b_banks[c]))
 
-        fb_sb = kept("fb_sb", [P, S * PACK], F32)
+        fb_sb = [kept("fb_sb%d" % c, [P, BLK, PACK], F32) for c in range(NBLK)]
         for c in range(NBLK):
             bank = psum.tile([P, PACK, BLK], F32, name="bank")
             for t in range(PACK):
                 for a in range(PASSES):
                     first_stage_pass(bank, *fp8_side(w1_q, a, t), a, c, t, a == 0, a == PASSES - 1)
-            nc.vector.tensor_tensor(block(fb_sb, c), woven(bank), block(b_sb, c), ALU.mult)
+            nc.vector.tensor_tensor(fb_sb[c][:], woven(bank), b_sb[c][:], ALU.mult)
 
+        w3_g = [stage.tile([P, PACK * H], BF16, name="w3_g%d" % a, offset=4096 * a, align_bytes=64)
+                for a in range(PASSES)]
         round_weight(nc.scalar.copy, w3_g[0], w3_raw0, 0, H)
         round_weight(nc.scalar.copy, w3_g[1], w3_raw1a, 0, H // 2)
         round_weight(nc.scalar.copy, w3_g[1], w3_raw1b, H // 2, H)
-        w3_q = [quantise("w3q0", w3_g[0][:], H), quantise("w3q1", w3_g[1][:], H)]
-
-        v2_w = kept("v2_w", [P, S2], U32)
+        w3_q = [quantise("w3q%d" % a, w3_g[a][:], H) for a in range(PASSES)]
+        v2_w = [shared.tile([P, HALF], U32, name="v2_w0", offset=0, align_bytes=64),
+                stage.tile([P, HALF], U32, name="v2_w1", offset=2048 * 7, align_bytes=64)]
         for h in range(2):
-            nc.vector.tensor_copy(v2_w[:, h * HALF:(h + 1) * HALF],
-                                  tab2_w[:].indirect(offs2_sb[:, h * 32:(h + 1) * 32]))
+            nc.vector.tensor_copy(v2_w[h][:], tab2_w[:].indirect(offs2_sb[:, h * 32:(h + 1) * 32]))
 
         d_banks = []
         for c in range(NBLK):
@@ -200,46 +202,58 @@ def tile_list_cousin_segment_scores_kernel(
             bank = d_banks[c]
             for t in range(PACK):
                 first_stage_pass(bank, *fp8_side(w3_q, 1, t), 1, c, t, False, t == PACK - 1)
-            nc.vector.tensor_tensor(block(h_g[c // 4], c % 4), woven(bank), block(fb_sb, c), ALU.max)
+            nc.vector.tensor_tensor(block(h_g[c // 4], c % 4), woven(bank), fb_sb[c][:], ALU.max)
             if c % 4 == 3:
                 h_q.append(quantise("hq%d" % (c // 4), h_g[c // 4][:], HALF))
 
         neg_temp = kept("neg_temp", [P, MT], F32)
-        nc.scalar.mul(neg_temp[:], temp_sb[:], -1.0)
+        nc.gpsimd.tensor_scalar(out=neg_temp[:], in0=temp_sb[:], scalar1=-1.0, scalar2=0.0,
+                                op0=ALU.mult, op1=ALU.add)
         top_half = kept("top_half", [P, MT], F32)
         top = kept("top", [P, MT], F32)
         bias = kept("bias", [P, MT], F32)
 
-        def scores(m):
-            rows = slice(m * P, (m + 1) * P)
+        e_sb = [kept("e_sb%d" % m, [P, S], F32) for m in range(MT)]
+
+        def scores(m, h):
             col = slice(m, m + 1)
-            e_sb = kept("e_sb%d" % m, [P, S], F32)
-            for h in range(2):
-                bank = psum.tile([P, HALF], F32, name="bank")
-                nc.tensor.matmul_mx(out=bank[:], lhsT=v2_w[:, rows].bitcast(FP8X4), lhsT_scale=v2_s[:, rows],
-                                    rhs=h_q[h][0][:].bitcast(FP8X4), rhs_scale=h_q[h][1][:],
-                                    start=True, stop=True)
-                nc.vector.tensor_scalar(out=e_sb[:, h * HALF:(h + 1) * HALF], in0=bank[:], scalar1=1.0,
-                                        scalar2=None if h == 0 else top_half[:, col],
-                                        op0=ALU.mult, op1=ALU.max,
-                                        accum_out=(top_half if h == 0 else top)[:, col])
+            bank = psum.tile([P, HALF], F32, name="bank")
+            nc.tensor.matmul_mx(out=bank[:], lhsT=v2_w[m // 4][:, m % 4 * P:(m % 4 + 1) * P].bitcast(FP8X4),
+                                lhsT_scale=v2_s[:, m * P:(m + 1) * P],
+                                rhs=h_q[h][0][:].bitcast(FP8X4), rhs_scale=h_q[h][1][:],
+                                start=True, stop=True)
+            nc.vector.tensor_scalar(out=e_sb[m][:, h * HALF:(h + 1) * HALF], in0=bank[:], scalar1=1.0,
+                                    scalar2=None if h == 0 else top_half[:, col],
+                                    op0=ALU.mult, op1=ALU.max,
+                                    accum_out=(top_half if h == 0 else top)[:, col])
+
+        def look_up(m):
+            col = slice(m, m + 1)
             nc.scalar.activation(out=bias[:, col], in_=top[:, col], func=ACT.Copy, scale=neg_temp[:, col])
             look = ring.tile([P, NP], F32, name="look")
-            nc.scalar.activation(out=look[:], in_=e_sb[:].indirect(pos1_sb[:]), func=ACT.Exp,
+            nc.scalar.activation(out=look[:], in_=e_sb[m][:].indirect(pos1_sb[:]), func=ACT.Exp,
                                  bias=bias[:, col], scale=temp_sb[:, col])
-            return e_sb, look
+            return look
 
-        def features(m, e_sb, look):
-            prod = ring.tile([P, NP], F32, name="prod")
-            nc.vector.tensor_tensor(prod[:], e_sb[:].indirect(pos2_sb[:]), look[:], ALU.mult)
-            res = ring.tile([P, NP], F32, name="res")
-            nc.scalar.activation(out=res[:], in_=prod[:], func=ACT.Identity, scale=5.0,
-                                 bias=lean_sb[:, m:m + 1])
-            nc.sync.dma_start(out[m * P:(m + 1) * P, :], res[:])
+        def features(m, look, pieces):
+            width = NP // pieces
+            for i in range(pieces):
+                cols = slice(i * width, (i + 1) * width)
+                prod = ring.tile([P, width], F32, name="prod")
+                nc.vector.tensor_tensor(prod[:], e_sb[m][:].indirect(pos2_sb[:, i * width // 16:(i + 1) * width // 16]),
+                                        look[:, cols], ALU.mult)
+                res = ring.tile([P, width], F32, name="res")
+                nc.scalar.activation(out=res[:], in_=prod[:], func=ACT.Identity, scale=5.0,
+                                     bias=lean_sb[:, m:m + 1])
+                nc.sync.dma_start(out[m * P:(m + 1) * P, cols], res[:])
 
-        pending = scores(0)
-        for m in range(1, MT):
-            ahead = scores(m)
-            features(m - 1, *pending)
-            pending = ahead
-        features(MT - 1, *pending)
+        scores(0, 0)
+        looks = []
+        for m in range(MT):
+            if m + 1 < MT:
+                scores(m + 1, 0)
+            scores(m, 1)
+            looks.append(look_up(m))
+            if m > 0:
+                features(m - 1, looks[m - 1], 1)
+        features(MT - 1, looks[MT - 1], 2)

@@ -158,7 +158,7 @@ def tile_list_cousin_segment_scores_kernel(
         def block(tile_, c):
             return tile_[:, c * BLK * PACK:(c + 1) * BLK * PACK].rearrange("p (n t) -> p n t", t=PACK)
 
-        b_sb = [stage.tile([P, BLK, PACK], F32, name="b_sb%d" % c, offset=2048 * c, align_bytes=64)
+        b_sb = [stage.tile([P, BLK, PACK], F32, name="b_sb%d" % c, offset=2048 * (c + 1), align_bytes=64)
                 for c in range(NBLK)]
         b_banks = []
         for c in range(NBLK):
@@ -186,7 +186,7 @@ def tile_list_cousin_segment_scores_kernel(
         round_weight(nc.scalar.copy, w3_g[1], w3_raw1b, H // 2, H)
         w3_q = [quantise("w3q%d" % a, w3_g[a][:], H) for a in range(PASSES)]
         v2_w = [shared.tile([P, HALF], U32, name="v2_w0", offset=0, align_bytes=64),
-                stage.tile([P, HALF], U32, name="v2_w1", offset=2048 * 7, align_bytes=64)]
+                stage.tile([P, HALF], U32, name="v2_w1", offset=2048 * 8, align_bytes=64)]
         for h in range(2):
             nc.vector.tensor_copy(v2_w[h][:], tab2_w[:].indirect(offs2_sb[:, h * 32:(h + 1) * 32]))
 
@@ -198,14 +198,6 @@ def tile_list_cousin_segment_scores_kernel(
             d_banks.append(bank)
         h_g = [kept("h_g%d" % h, [P, HALF * PACK], BF16) for h in range(2)]
         h_q = []
-        for c in range(NBLK):
-            bank = d_banks[c]
-            for t in range(PACK):
-                first_stage_pass(bank, *fp8_side(w3_q, 1, t), 1, c, t, False, t == PACK - 1)
-            nc.vector.tensor_tensor(block(h_g[c // 4], c % 4), woven(bank), fb_sb[c][:], ALU.max)
-            if c % 4 == 3:
-                h_q.append(quantise("hq%d" % (c // 4), h_g[c // 4][:], HALF))
-
         neg_temp = kept("neg_temp", [P, MT], F32)
         nc.gpsimd.tensor_scalar(out=neg_temp[:], in0=temp_sb[:], scalar1=-1.0, scalar2=0.0,
                                 op0=ALU.mult, op1=ALU.add)
@@ -247,13 +239,22 @@ def tile_list_cousin_segment_scores_kernel(
                                      bias=lean_sb[:, m:m + 1])
                 nc.sync.dma_start(out[m * P:(m + 1) * P, cols], res[:])
 
+        for c in range(NBLK):
+            bank = d_banks[c]
+            for t in range(PACK):
+                first_stage_pass(bank, *fp8_side(w3_q, 1, t), 1, c, t, False, t == PACK - 1)
+            nc.vector.tensor_tensor(block(h_g[c // 4], c % 4), woven(bank), fb_sb[c][:], ALU.max)
+            if c == 4:
+                h_q.append(quantise("hq0", h_g[0][:], HALF))
         scores(0, 0)
+        h_q.append(quantise("hq1", h_g[1][:], HALF))
         looks = []
         for m in range(MT):
             if m + 1 < MT:
                 scores(m + 1, 0)
             scores(m, 1)
             looks.append(look_up(m))
-            if m > 0:
-                features(m - 1, looks[m - 1], 1)
+            if m > 1:
+                features(m - 2, looks[m - 2], 1)
+        features(MT - 2, looks[MT - 2], 1)
         features(MT - 1, looks[MT - 1], 2)

from contextlib import ExitStack

import concourse.mybir as mybir

K, H, T, S, T3, S2, NP = 1024, 512, 4096, 1024, 2048, 1024, 512
FLOPS = 2 * (3 * K * H * S + H * S2 * S)

F32 = mybir.dt.float32
BF16 = mybir.dt.bfloat16
I32 = mybir.dt.int32
U32 = mybir.dt.uint32
U16 = mybir.dt.uint16
U8 = mybir.dt.uint8
FP8X4 = mybir.dt.float8_e4m3fn_x4
FP4X4 = mybir.dt.float4_e2m1fn_x4
ALU = mybir.AluOpType
ACT = mybir.ActivationFunctionType

P = 128
PACK = 4
PASSES = K // (P * PACK)
BLK = 128
NBLK = S // BLK
HALF = 512
MT = S2 // P


def tile_list_cousin_segment_scores_kernel(
    tc, tab_words, tab_scales, offs, tab2_words, tab2_scales, offs2, pos1, pos2,
    w1, w2_words, w2_scales, w3, temp, lean, out,
):
    nc = tc.nc
    with ExitStack() as ctx:
        lists = ctx.enter_context(tc.tile_pool(name="lists", bufs=1))
        keep = ctx.enter_context(tc.tile_pool(name="keep", bufs=1))
        shared = ctx.enter_context(tc.tile_pool(name="shared", bufs=1))
        stage = ctx.enter_context(tc.tile_pool(name="stage", bufs=1))
        ring = ctx.enter_context(tc.tile_pool(name="ring", bufs=4))
        psum = ctx.enter_context(tc.psum_pool(name="psum", bufs=8))

        def kept(name, shape, dtype):
            return keep.tile(shape, dtype, name=name, align_bytes=64)

        offs_sb = lists.tile([P, S // 16], U16, name="offs_sb")
        offs2_sb = lists.tile([P, S2 // 16], U16, name="offs2_sb")
        pos1_sb = lists.tile([P, NP // 16], U16, name="pos1_sb")
        pos2_sb = lists.tile([P, NP // 16], U16, name="pos2_sb")

        tab_w = [kept("tab_w0", [P, T], U32), shared.tile([P, T], U32, name="tab_w1", offset=0)]
        tab_s = kept("tab_s", [P, T], U8)
        tab2_w = kept("tab2_w", [P, T3], U32)
        tab2_s = kept("tab2_s", [P, T3], U8)
        w2_w_raw = kept("w2_w_raw", [P, PASSES, 2 * H], U8)
        w2_s_raw = kept("w2_s_raw", [P, PASSES, H], U8)
        v_s1 = kept("v_s1", [P, S], U8)

        nc.vector.memset(tab_s[:].bitcast(I32), 0)
        nc.vector.memset(tab2_s[:].bitcast(I32), 0)
        nc.vector.memset(w2_s_raw[:].bitcast(I32), 0)
        nc.vector.memset(v_s1[:].bitcast(I32), 0)

        def load_words(dst, src, c0, c1):
            nc.sync.dma_start(dst[:, c0:c1].bitcast(I32),
                              src[:, c0:c1, :].rearrange("p t i -> p (t i)").bitcast(I32))

        def load_weight(name, w, a, c0, c1):
            raw = kept(name, [P, PACK, c1 - c0], F32)
            rows = w[a * P * PACK:(a + 1) * P * PACK, c0:c1]
            nc.sync.dma_start(raw[:], rows.rearrange("(p j) c -> p j c", j=PACK))
            return raw

        def load_scale_rows(dst, src):
            nc.sync.dma_start(dst.bitcast(I32), src.bitcast(I32))

        def load_w2_scales(q):
            load_scale_rows(w2_s_raw[32 * q:32 * q + 4, :, :],
                            w2_scales[:, 4 * q:4 * q + 4, :].rearrange("a r c -> r a c"))

        nc.sync.dma_start(offs_sb[:], offs)
        nc.sync.dma_start(w2_w_raw[:].bitcast(I32), w2_words.rearrange("a p c -> p a c").bitcast(I32))
        nc.sync.dma_start(offs2_sb[:], offs2)
        nc.sync.dma_start(pos1_sb[:], pos1)
        nc.sync.dma_start(pos2_sb[:], pos2)
        for q in range(3):
            load_words(tab_w[0], tab_words[0], q * T // 16, (q + 1) * T // 16)
        for r in range(4):
            load_scale_rows(tab_s[r:P:16, :], tab_scales[:, r:16:4, :].rearrange("a q t -> q a t"))
        load_words(tab_w[0], tab_words[0], 3 * T // 16, T)
        for q in range(4):
            load_w2_scales(q)
        w1_raw0 = load_weight("w1_raw0", w1, 0, 0, H)
        for q in range(4):
            load_scale_rows(tab2_s[32 * q:32 * q + 4, :], tab2_scales[0, 4 * q:4 * q + 4, :])
        load_words(tab_w[1], tab_words[1], 0, T // 2)
        w2_w = kept("w2_w", [P, PASSES, 2 * H], U8)
        w2_s = kept("w2_s", [P, PASSES, H], U8)
        nc.vector.tensor_copy(w2_w[:].bitcast(U16).rearrange("p a (t m) -> p a t m", t=PACK),
                              w2_w_raw[:].bitcast(U16).rearrange("p a (m t) -> p a t m", t=PACK))
        v_s0 = kept("v_s0", [P, S], U8)
        nc.vector.tensor_copy(v_s0[:], tab_s[:].indirect(offs_sb[:]))
        nc.sync.dma_start(v_s1[0:P - 16, :].bitcast(I32), v_s0[16:P, :].bitcast(I32))
        load_words(tab_w[1], tab_words[1], T // 2, T)
        w1_raw1 = load_weight("w1_raw1", w1, 1, 0, H)
        load_words(tab2_w, tab2_words[0], 0, T3)
        w3_raw0 = load_weight("w3_raw0", w3, 0, 0, H)
        w3_raw1a = load_weight("w3_raw1a", w3, 1, 0, H // 2)
        w3_raw1b = load_weight("w3_raw1b", w3, 1, H // 2, H)
        temp_sb = kept("temp_sb", [P, MT], F32)
        lean_sb = kept("lean_sb", [P, MT], F32)
        with nc.allow_non_contiguous_dma(reason="one value a row, rows on partitions"):
            nc.sync.dma_start(temp_sb[:], temp.rearrange("(c p) -> p c", p=P))
            nc.sync.dma_start(lean_sb[:], lean.rearrange("(c p) -> p c", p=P))

        def round_weight(copy, grouped, raw, c0, c1):
            dst = grouped[:].rearrange("p (t m j) -> p m j t", t=PACK, j=PACK)[:, c0 // PACK:c1 // PACK]
            copy(dst, raw[:].rearrange("p j (m t) -> p m j t", t=PACK))

        def quantise(name, grouped, width):
            codes = kept(name + "_c", [P, width], U32)
            scales = kept(name + "_s", [P, width], U8)
            nc.vector.quantize_mx(out=codes[:].bitcast(FP8X4), scales=scales[:], in_=grouped)
            return codes, scales

        v_s = [v_s0, v_s1]
        v_w = [kept("v_w%d" % a, [P, S], U32) for a in range(PASSES)]
        nc.vector.tensor_copy(v_w[0][:], tab_w[0][:].indirect(offs_sb[:]))
        nc.vector.tensor_copy(w2_s[:].rearrange("p a (t m) -> p a t m", t=PACK),
                              w2_s_raw[:].rearrange("p a (m t) -> p a t m", t=PACK))
        v2_s = kept("v2_s", [P, S2], U8)
        nc.vector.tensor_copy(v2_s[:], tab2_s[:].indirect(offs2_sb[:]))

        w1_g = [kept("w1_g0", [P, PACK * H], BF16),
                shared.tile([P, PACK * H], BF16, name="w1_g1", offset=0, align_bytes=64)]
        round_weight(nc.scalar.copy, w1_g[0], w1_raw0, 0, H)
        w1_q = [quantise("w1q0", w1_g[0][:], H)]
        for h in range(2):
            nc.vector.tensor_copy(v_w[1][:, h * HALF:(h + 1) * HALF],
                                  tab_w[1][:].indirect(offs_sb[:, h * 32:(h + 1) * 32]))
        round_weight(nc.vector.tensor_copy, w1_g[1], w1_raw1, 0, H)
        w1_q.append(quantise("w1q1", w1_g[1][:], H))

        def first_stage_pass(bank, codes, scales, a, c, t, start, stop):
            cols = slice(c * BLK, (c + 1) * BLK)
            nc.tensor.matmul_mx(out=bank[:, t, :], lhsT=codes, lhsT_scale=scales,
                                rhs=v_w[a][:, cols].bitcast(FP8X4),
                                rhs_scale=v_s[a][:, cols],
                                start=start, stop=stop)

        def fp8_side(q, a, t):
            return q[a][0][:, t * P:(t + 1) * P].bitcast(FP8X4), q[a][1][:, t * P:(t + 1) * P]

        def fp4_side(a, t):
            return w2_w[:, a, 2 * t * P:2 * (t + 1) * P].bitcast(FP4X4), w2_s[:, a, t * P:(t + 1) * P]

        def woven(bank):
            return bank[:].rearrange("p t n -> p n t")

        def block(tile_, c):
            return tile_[:, c * BLK * PACK:(c + 1) * BLK * PACK].rearrange("p (n t) -> p n t", t=PACK)

        b_sb = [stage.tile([P, BLK, PACK], F32, name="b_sb%d" % c, offset=2048 * (c + 1), align_bytes=64)
                for c in range(NBLK)]
        b_banks = []
        for c in range(NBLK):
            bank = psum.tile([P, PACK, BLK], F32, name="bank")
            for t in range(PACK):
                first_stage_pass(bank, *fp4_side(0, t), 0, c, t, t == 0, False)
            b_banks.append(bank)
        for c in range(NBLK):
            for t in range(PACK):
                first_stage_pass(b_banks[c], *fp4_side(1, t), 1, c, t, False, t == PACK - 1)
            nc.scalar.copy(b_sb[c][:], woven(b_banks[c]))

        fb_sb = [kept("fb_sb%d" % c, [P, BLK, PACK], F32) for c in range(NBLK)]
        for c in range(NBLK):
            bank = psum.tile([P, PACK, BLK], F32, name="bank")
            for t in range(PACK):
                for a in range(PASSES):
                    first_stage_pass(bank, *fp8_side(w1_q, a, t), a, c, t, a == 0, a == PASSES - 1)
            nc.vector.tensor_tensor(fb_sb[c][:], woven(bank), b_sb[c][:], ALU.mult)

        w3_g = [stage.tile([P, PACK * H], BF16, name="w3_g%d" % a, offset=4096 * a, align_bytes=64)
                for a in range(PASSES)]
        round_weight(nc.scalar.copy, w3_g[0], w3_raw0, 0, H)
        round_weight(nc.scalar.copy, w3_g[1], w3_raw1a, 0, H // 2)
        round_weight(nc.scalar.copy, w3_g[1], w3_raw1b, H // 2, H)
        w3_q = [quantise("w3q%d" % a, w3_g[a][:], H) for a in range(PASSES)]
        v2_w = [shared.tile([P, HALF], U32, name="v2_w0", offset=0, align_bytes=64),
                stage.tile([P, HALF], U32, name="v2_w1", offset=2048 * 8, align_bytes=64)]
        for h in range(2):
            nc.vector.tensor_copy(v2_w[h][:], tab2_w[:].indirect(offs2_sb[:, h * 32:(h + 1) * 32]))

        d_banks = []
        for c in range(NBLK):
            bank = psum.tile([P, PACK, BLK], F32, name="bank")
            for t in range(PACK):
                first_stage_pass(bank, *fp8_side(w3_q, 0, t), 0, c, t, t == 0, False)
            d_banks.append(bank)
        h_g = [kept("h_g%d" % h, [P, HALF * PACK], BF16) for h in range(2)]
        h_q = []
        neg_temp = kept("neg_temp", [P, MT], F32)
        nc.gpsimd.tensor_scalar(out=neg_temp[:], in0=temp_sb[:], scalar1=-1.0, scalar2=0.0,
                                op0=ALU.mult, op1=ALU.add)
        top_half = kept("top_half", [P, MT], F32)
        top = kept("top", [P, MT], F32)
        bias = kept("bias", [P, MT], F32)

        e_sb = [kept("e_sb%d" % m, [P, S], F32) for m in range(MT)]

        def scores(m, h):
            col = slice(m, m + 1)
            bank = psum.tile([P, HALF], F32, name="bank")
            nc.tensor.matmul_mx(out=bank[:], lhsT=v2_w[m // 4][:, m % 4 * P:(m % 4 + 1) * P].bitcast(FP8X4),
                                lhsT_scale=v2_s[:, m * P:(m + 1) * P],
                                rhs=h_q[h][0][:].bitcast(FP8X4), rhs_scale=h_q[h][1][:],
                                start=True, stop=True)
            nc.vector.tensor_scalar(out=e_sb[m][:, h * HALF:(h + 1) * HALF], in0=bank[:], scalar1=1.0,
                                    scalar2=None if h == 0 else top_half[:, col],
                                    op0=ALU.mult, op1=ALU.max,
                                    accum_out=(top_half if h == 0 else top)[:, col])

        def look_up(m):
            col = slice(m, m + 1)
            nc.scalar.activation(out=bias[:, col], in_=top[:, col], func=ACT.Copy, scale=neg_temp[:, col])
            look = ring.tile([P, NP], F32, name="look")
            nc.scalar.activation(out=look[:], in_=e_sb[m][:].indirect(pos1_sb[:]), func=ACT.Exp,
                                 bias=bias[:, col], scale=temp_sb[:, col])
            return look

        def features(m, look, pieces):
            width = NP // pieces
            for i in range(pieces):
                cols = slice(i * width, (i + 1) * width)
                prod = ring.tile([P, width], F32, name="prod")
                nc.vector.tensor_tensor(prod[:], e_sb[m][:].indirect(pos2_sb[:, i * width // 16:(i + 1) * width // 16]),
                                        look[:, cols], ALU.mult)
                res = ring.tile([P, width], F32, name="res")
                nc.scalar.activation(out=res[:], in_=prod[:], func=ACT.Identity, scale=5.0,
                                     bias=lean_sb[:, m:m + 1])
                nc.sync.dma_start(out[m * P:(m + 1) * P, cols], res[:])

        for c in range(NBLK):
            bank = d_banks[c]
            for t in range(PACK):
                first_stage_pass(bank, *fp8_side(w3_q, 1, t), 1, c, t, False, t == PACK - 1)
            nc.vector.tensor_tensor(block(h_g[c // 4], c % 4), woven(bank), fb_sb[c][:], ALU.max)
            if c == 4:
                h_q.append(quantise("hq0", h_g[0][:], HALF))
        scores(0, 0)
        h_q.append(quantise("hq1", h_g[1][:], HALF))
        looks = []
        for m in range(MT):
            if m + 1 < MT:
                scores(m + 1, 0)
            scores(m, 1)
            looks.append(look_up(m))
            if m > 1:
                features(m - 2, looks[m - 2], 1)
        features(MT - 2, looks[MT - 2], 1)
        features(MT - 1, looks[MT - 1], 2)
